import numpy as np
import ml_dtypes


def mxq(x, axis, fmt="e4m3"):
    dtype, down = {"e4m3": (ml_dtypes.float8_e4m3fn, 7), "e5m2": (ml_dtypes.float8_e5m2, 14)}[fmt]
    v = np.moveaxis(np.asarray(x, np.float32).astype(ml_dtypes.bfloat16).astype(np.float64), axis, -1)
    blocks = v.reshape(v.shape[:-1] + (-1, 32))
    amax = np.abs(blocks).max(-1, keepdims=True)
    byte = np.maximum(np.where(amax > 0, np.frexp(amax)[1] - 1 + 127, 0) - down, 1)
    scale = np.exp2(byte - 127.0)
    codes = (blocks / scale).astype(np.float32).astype(dtype).astype(np.float64)
    return np.moveaxis((codes * scale).reshape(v.shape), -1, axis)


WIDE = False


def mx_kscale(k):
    if not WIDE:
        return np.ones(k)
    levels = np.array([10, -10, 5, -5, 0])
    if k % 512:
        return np.exp2(np.random.permutation(np.resize(levels, k // 32))).repeat(32)
    a = np.empty((k // 512, 16))
    for p in range(k // 512):
        a[p, :8] = np.random.permutation(np.resize(levels, 8))
        for g in range(8):
            far = levels[np.abs(levels - a[p, g]) >= 10]
            a[p, g + 8] = far[np.random.randint(len(far))]
    return np.exp2(a.ravel()).repeat(32)


def f64(x):
    return np.asarray(x).astype(np.float64)


def striped(idx):
    return np.tile(np.asarray(idx).reshape(-1, 16).T, (8, 1)).astype(np.uint16)


def unstriped(offs):
    return offs[:16].T.reshape(-1).astype(np.int64)


E2M1 = np.array([0.0, 0.5, 1.0, 1.5, 2.0, 3.0, 4.0, 6.0, -0.0, -0.5, -1.0, -1.5, -2.0, -3.0, -4.0, -6.0])


def pack_weight(w, fmt):
    k, n = w.shape
    w = f64(np.asarray(w, np.float32).astype(ml_dtypes.bfloat16)).reshape(k // 32, 32, n)
    amax = np.abs(w).max(1)
    if fmt == "e4m3":
        byte = np.frexp(amax)[1] - 1 + 127 - 7
    else:
        mant, ex = np.frexp(amax / 6.0)
        byte = np.where(mant > 0.5, ex, ex - 1) + 127
    byte = np.clip(np.where(amax > 0, byte, 1), 1, 254)
    scaled = (w * np.exp2(127.0 - byte)[:, None, :]).reshape(k, n).astype(np.float32)
    by_word = np.ascontiguousarray(scaled.reshape(k // 512, 128, 4, n).transpose(0, 1, 3, 2))
    if fmt == "e4m3":
        words = by_word.astype(ml_dtypes.float8_e4m3fn).view(np.uint8)
    else:
        c = by_word.astype(ml_dtypes.float4_e2m1fn).view(np.uint8) & 0xF
        words = (c[..., 0::2] | (c[..., 1::2] << 4)).reshape(k // 512, 128, 2 * n)
    return np.ascontiguousarray(words), np.ascontiguousarray(byte.astype(np.uint8).reshape(k // 512, 16, n))


def unpack_weight(words, scales, fmt):
    g, _, n = scales.shape
    words = np.ascontiguousarray(words).reshape(g, 128, n, -1)
    if fmt == "e4m3":
        vals = words.view(ml_dtypes.float8_e4m3fn).astype(np.float64)
    else:
        nib = np.empty((g, 128, n, 4), np.uint8)
        nib[..., 0::2] = words & 0xF
        nib[..., 1::2] = words >> 4
        vals = E2M1[nib]
    vals = vals * np.repeat(np.exp2(scales.astype(np.float64) - 127.0), 8, axis=1)[..., None]
    return vals.transpose(0, 1, 3, 2).reshape(g * 512, n)


D, E, T, I, Q, G = 512, 512, 2048, 512, 128, 32


def setup_inputs():
    n = np.random.standard_normal
    idx = np.random.permutation(T)[:I]
    fd = mx_kscale(D)
    fe = mx_kscale(E)
    keysp = pack_weight(n((D, T)) / fd[:, None], "e2m1")
    valsp = pack_weight(n((E, T)) / fe[:, None], "e2m1")
    return {
        "query": (n((D, Q)) * 0.8 / np.sqrt(D) * fd[:, None]).astype(np.float32),
        "keys_words": keysp[0],
        "keys_scales": keysp[1],
        "gout": (n((E, Q)) * 1 / np.sqrt(E) * fe[:, None]).astype(np.float32),
        "vals_words": valsp[0],
        "vals_scales": valsp[1],
        "old": (0.5 * n((Q, T))).astype(np.float32),
        "offs": striped(idx),
    }


def reference(query, keys_words, keys_scales, gout, vals_words, vals_scales, old, offs):
    idx = unstriped(offs)
    keysu = unpack_weight(keys_words, keys_scales, "e2m1")
    valsu = unpack_weight(vals_words, vals_scales, "e2m1")
    queryq = mxq(f64(query), 0, "e4m3")
    keysidxg = keysu[:, idx]
    a = queryq.T @ keysidxg
    m1 = a.reshape(Q, G, I // G).mean(axis=2)
    mr = np.repeat(m1, I // G, axis=1)
    ce = a - mr
    v1 = np.sqrt(np.square(ce).reshape(Q, G, I // G).mean(axis=2) + 0.3)
    vr = np.repeat(v1, I // G, axis=1)
    s = ce / vr
    p = np.exp(s - np.max(s, axis=1, keepdims=True))
    z = np.sum(p, axis=1, keepdims=True)
    goutq = mxq(f64(gout), 0, "e4m3")
    valsidxg = valsu[:, idx]
    c0 = goutq.T @ valsidxg
    dz = np.sum(c0 * p / np.square(z) * (-1.0), axis=1, keepdims=True)
    dp = c0 / z + dz
    ds = dp * p
    dvr = ds * ce / np.square(vr) * (-1.0)
    dv1 = dvr.reshape(Q, G, I // G).sum(axis=2)
    e1 = dv1 * 0.5 / np.sqrt(np.square(ce).reshape(Q, G, I // G).mean(axis=2) + 0.3) / 16.0
    r1 = np.repeat(e1, I // G, axis=1)
    dce = ds / vr + r1 * ce * 2.0
    dmr = dce * (-1.0)
    dm1 = dmr.reshape(Q, G, I // G).sum(axis=2)
    e2 = dm1 / 16.0
    r2 = np.repeat(e2, I // G, axis=1)
    da = dce + r2
    gs = da * 512.0
    gf = np.zeros((Q, T))
    gf[:, idx] = gs
    y = f64(old) + gf
    return y

@@ -1,0 +1,172 @@
+from contextlib import ExitStack
+
+import concourse.mybir as mybir
+
+D, E, T, I, Q, G = 512, 512, 2048, 512, 128, 32
+FLOPS = 2 * Q * I * (D + E)
+
+F32 = mybir.dt.float32
+BF16 = mybir.dt.bfloat16
+I32 = mybir.dt.int32
+U32 = mybir.dt.uint32
+U16 = mybir.dt.uint16
+U8 = mybir.dt.uint8
+FP8X4 = mybir.dt.float8_e4m3fn_x4
+FP4X4 = mybir.dt.float4_e2m1fn_x4
+ALU = mybir.AluOpType
+ACT = mybir.ActivationFunctionType
+AX = mybir.AxisListType
+
+P = 128
+PACK = 4
+PAGE = I // G
+HALF = I // 2
+QUARTER = I // 4
+STORE = 512
+
+
+def tile_attend_bpagestandard_s_kernel(tc, query, keys_words, keys_scales, gout, vals_words, vals_scales, old, offs, out):
+    nc = tc.nc
+
+    with ExitStack() as ctx:
+        sb = ctx.enter_context(tc.tile_pool(name="sb", bufs=1))
+        ps = ctx.enter_context(tc.psum_pool(name="ps", bufs=1))
+
+        def slots(lo, n):
+            return slice(lo, lo + n)
+
+        def pages(lo, n):
+            return slice(lo // PAGE, (lo + n) // PAGE)
+
+        def paged(ap):
+            return ap.rearrange("p (g j) -> p g j", j=PAGE)
+
+        def spread(ap):
+            return ap.unsqueeze(2).to_broadcast([P, ap.shape[1], PAGE])
+
+        offsets = sb.tile([P, I // 16], U16, name="offsets")
+
+        def listed(window, lo, n):
+            return window[:].indirect(offsets[:, lo // 16 : (lo + n) // 16])
+
+        key_bytes = sb.tile([P, T], U8, name="key_bytes", align_bytes=64)
+        val_bytes = sb.tile([P, T], U8, name="val_bytes", align_bytes=64)
+        key_words = sb.tile([P, T], U16, name="key_words", align_bytes=64)
+        val_words = sb.tile([P, T], U16, name="val_words", align_bytes=64)
+        q_raw = sb.tile([P, PACK, Q], F32, name="q_raw")
+        g_raw = sb.tile([P, PACK, Q], F32, name="g_raw")
+        window = sb.tile([P, T], F32, name="window")
+        warm = sb.tile([P, 2], F32, name="warm")
+
+        nc.gpsimd.memset(key_bytes[:].bitcast(I32), 0)
+        nc.gpsimd.memset(warm[:, 0:1], 1.0)
+        nc.vector.memset(val_bytes[:].bitcast(I32), 0)
+        nc.vector.memset(window[:], 0.0)
+
+        def load_scale_rows(queue, tile, rows):
+            for f in range(4):
+                queue.dma_start(out=tile[32 * f : 32 * f + 4, :].bitcast(I32), in_=rows[0, 4 * f : 4 * f + 4, :].bitcast(I32))
+
+        nc.sync.dma_start(offsets[:], offs)
+        load_scale_rows(nc.scalar, key_bytes, keys_scales)
+        nc.scalar.activation(out=warm[:, 1:2], in_=warm[:, 0:1], func=ACT.Abs_reciprocal_sqrt)
+        nc.sync.dma_start(out=q_raw[:], in_=query.rearrange("(p j) w -> p j w", j=PACK))
+        nc.sync.dma_start(out=key_words[:].bitcast(I32), in_=keys_words[0].bitcast(I32))
+        nc.sync.dma_start(out=val_words[:].bitcast(I32), in_=vals_words[0].bitcast(I32))
+        nc.sync.dma_start(out=g_raw[:], in_=gout.rearrange("(p j) w -> p j w", j=PACK))
+        load_scale_rows(nc.sync, val_bytes, vals_scales)
+        olds = []
+        for c in range(T // STORE):
+            old_c = sb.tile([P, STORE], F32, name="old%d" % c)
+            nc.sync.dma_start(out=old_c[:], in_=old[:, slots(c * STORE, STORE)])
+            olds.append(old_c)
+
+        def quantise(raw, name):
+            grouped = sb.tile([P, Q, PACK], BF16, name=name + "_grouped", align_bytes=64)
+            codes = sb.tile([P, Q], U32, name=name + "_codes", align_bytes=64)
+            scales = sb.tile([P, Q], U8, name=name + "_scales", align_bytes=64)
+            nc.scalar.copy(out=grouped[:], in_=raw[:].rearrange("p j w -> p w j"))
+            nc.vector.quantize_mx(out=codes[:].bitcast(FP8X4), scales=scales[:], in_=grouped[:].rearrange("p w j -> p (w j)"))
+            return codes, scales
+
+        kw = sb.tile([P, I], U16, name="kw", align_bytes=64)
+        kb = sb.tile([P, I], U8, name="kb", align_bytes=64)
+        nc.vector.tensor_copy(kb[:], listed(key_bytes, 0, I))
+        q_codes, q_scales = quantise(q_raw, "q")
+        scores = []
+        for h in range(2):
+            sl = slots(h * HALF, HALF)
+            nc.vector.tensor_copy(kw[:, sl], listed(key_words, h * HALF, HALF))
+            a_h = ps.tile([P, HALF], F32, name="a%d" % h)
+            nc.tensor.matmul_mx(out=a_h[:], lhsT=q_codes[:].bitcast(FP8X4), lhsT_scale=q_scales[:],
+                                rhs=kw[:, sl].bitcast(FP4X4), rhs_scale=kb[:, sl], start=True, stop=True)
+            scores.append(a_h)
+
+        page_sum = sb.tile([P, G], F32, name="page_sum")
+        page_sq = sb.tile([P, G], F32, name="page_sq")
+        rinv = sb.tile([P, G], F32, name="rinv")
+        ce = sb.tile([P, I], F32, name="ce", tag="ce_vb", align_bytes=64)
+        sq = sb.tile([P, I], F32, name="sq")
+        s = sb.tile([P, I], F32, name="s")
+        p = sb.tile([P, I], F32, name="p")
+        halves = [(slots(h * HALF, HALF), pages(h * HALF, HALF)) for h in range(2)]
+        for h, (sl, pg) in enumerate(halves):
+            nc.vector.tensor_reduce(out=page_sum[:, pg], in_=paged(scores[h][:]), axis=AX.X, op=ALU.add)
+        for h, (sl, pg) in enumerate(halves):
+            nc.vector.scalar_tensor_tensor(out=paged(ce[:, sl]), in0=spread(page_sum[:, pg]), scalar=-1.0 / PAGE,
+                                           in1=paged(scores[h][:]), op0=ALU.mult, op1=ALU.add)
+            nc.scalar.activation(out=sq[:, sl], in_=ce[:, sl], func=ACT.Square)
+        for sl, pg in halves:
+            nc.vector.tensor_reduce(out=page_sq[:, pg], in_=paged(sq[:, sl]), axis=AX.X, op=ALU.add)
+            nc.scalar.activation(out=rinv[:, pg], in_=page_sq[:, pg], func=ACT.Abs_reciprocal_sqrt, scale=1.0 / PAGE, bias=0.3)
+        for sl, pg in halves:
+            nc.vector.tensor_tensor(out=paged(s[:, sl]), in0=paged(ce[:, sl]), in1=spread(rinv[:, pg]), op=ALU.mult)
+        neg_max = sb.tile([P, 1], F32, name="neg_max")
+        z = sb.tile([P, 1], F32, name="z")
+        nc.vector.tensor_reduce(out=neg_max[:], in_=s[:], axis=AX.X, op=ALU.max, negate=True)
+        nc.scalar.activation(out=p[:], in_=s[:], func=ACT.Exp, bias=neg_max[:], accum_out=z[:])
+
+        vw = sb.tile([P, I], U16, name="vw", align_bytes=64)
+        vb = sb.tile([P, I], U8, name="vb", tag="ce_vb", align_bytes=64)
+        for h, (sl, pg) in enumerate(halves):
+            nc.vector.tensor_copy(vw[:, sl], listed(val_words, h * HALF, HALF))
+        g_codes, g_scales = quantise(g_raw, "g")
+        for h, (sl, pg) in enumerate(halves):
+            nc.vector.tensor_copy(vb[:, sl], listed(val_bytes, h * HALF, HALF))
+        c0 = ps.tile([P, I], F32, name="c0")
+        nc.tensor.matmul_mx(out=c0[:], lhsT=g_codes[:].bitcast(FP8X4), lhsT_scale=g_scales[:],
+                            rhs=vw[:].bitcast(FP4X4), rhs_scale=vb[:], start=True, stop=True)
+
+        rz = sb.tile([P, 1], F32, name="rz")
+        cbar = sb.tile([P, 1], F32, name="cbar")
+        rk = sb.tile([P, G], F32, name="rk")
+        pr = sb.tile([P, I], F32, name="pr")
+        cp = sb.tile([P, I], F32, name="cp")
+        nc.vector.reciprocal(out=rz[:], in_=z[:])
+        nc.vector.tensor_scalar(out=rk[:], in0=rinv[:], scalar1=rz[:], scalar2=512.0, op0=ALU.mult, op1=ALU.mult)
+        nc.vector.tensor_tensor(out=paged(pr[:]), in0=paged(p[:]), in1=spread(rk[:]), op=ALU.mult)
+        nc.vector.scalar_tensor_tensor(out=cp[:], in0=c0[:], scalar=rz[:], in1=p[:], op0=ALU.mult, op1=ALU.mult, accum_out=cbar[:])
+
+        dt = sb.tile([P, 2, I], F32, name="dt")
+        sums = sb.tile([P, 2, G], F32, name="sums")
+        means = sb.tile([P, 2, G], F32, name="means")
+        y = sb.tile([P, I], F32, name="y")
+        for sl, pg in halves:
+            nc.vector.scalar_tensor_tensor(out=dt[:, 0, sl], in0=c0[:, sl], scalar=cbar[:], in1=pr[:, sl], op0=ALU.subtract, op1=ALU.mult)
+        for sl, pg in halves:
+            nc.vector.tensor_tensor(out=dt[:, 1, sl], in0=dt[:, 0, sl], in1=s[:, sl], op=ALU.mult)
+        for u in range(4):
+            sl, pg = slots(u * QUARTER, QUARTER), pages(u * QUARTER, QUARTER)
+            nc.vector.tensor_reduce(out=sums[:, :, pg], in_=dt[:, :, sl].rearrange("p k (g j) -> p k g j", j=PAGE), axis=AX.X, op=ALU.add)
+            nc.scalar.activation(out=means[:, :, pg], in_=sums[:, :, pg], func=ACT.Copy, scale=-1.0 / PAGE)
+            for g in range(pg.start, pg.stop):
+                one = slots(g * PAGE, PAGE)
+                nc.scalar.activation(out=y[:, one], in_=s[:, one], func=ACT.Identity, scale=means[:, 1, g : g + 1], bias=means[:, 0, g : g + 1])
+        for u in range(4):
+            sl = slots(u * QUARTER, QUARTER)
+            nc.vector.tensor_tensor(out=listed(window, u * QUARTER, QUARTER), in0=dt[:, 0, sl], in1=y[:, sl], op=ALU.add)
+
+        for c in range(T // STORE):
+            cols = slots(c * STORE, STORE)
+            nc.vector.tensor_tensor(out=olds[c][:], in0=window[:, cols], in1=olds[c][:], op=ALU.add)
+            nc.sync.dma_start(out=out[:, cols], in_=olds[c][:])

@@ -21,7 +21,7 @@ P = 128
 PACK = 4
 PAGE = I // G
 HALF = I // 2
-QUARTER = I // 4
+FIRST = 192
 STORE = 512
 
 
@@ -51,35 +51,30 @@ def tile_attend_bpagestandard_s_kernel(tc, query, keys_words, keys_scales, gout,
 
         key_bytes = sb.tile([P, T], U8, name="key_bytes", align_bytes=64)
         val_bytes = sb.tile([P, T], U8, name="val_bytes", align_bytes=64)
-        key_words = sb.tile([P, T], U16, name="key_words", align_bytes=64)
-        val_words = sb.tile([P, T], U16, name="val_words", align_bytes=64)
+        key_words = sb.tile([P, T], U16, name="key_words", tag="keys_old", align_bytes=64)
         q_raw = sb.tile([P, PACK, Q], F32, name="q_raw")
-        g_raw = sb.tile([P, PACK, Q], F32, name="g_raw")
         window = sb.tile([P, T], F32, name="window")
-        warm = sb.tile([P, 2], F32, name="warm")
+        warm = sb.tile([P, 2], F32, name="warm", tag="vals_old", align_bytes=64)
 
-        nc.gpsimd.memset(key_bytes[:].bitcast(I32), 0)
+        nc.vector.memset(key_bytes[:].bitcast(I32), 0)
         nc.gpsimd.memset(warm[:, 0:1], 1.0)
+        nc.gpsimd.memset(window[:], 0.0)
         nc.vector.memset(val_bytes[:].bitcast(I32), 0)
-        nc.vector.memset(window[:], 0.0)
 
         def load_scale_rows(queue, tile, rows):
             for f in range(4):
                 queue.dma_start(out=tile[32 * f : 32 * f + 4, :].bitcast(I32), in_=rows[0, 4 * f : 4 * f + 4, :].bitcast(I32))
 
         nc.sync.dma_start(offsets[:], offs)
-        load_scale_rows(nc.scalar, key_bytes, keys_scales)
+        load_scale_rows(nc.sync, key_bytes, keys_scales)
+        nc.scalar.dma_start(out=key_words[:].bitcast(I32), in_=keys_words[0].bitcast(I32))
+        nc.scalar.dma_start(out=q_raw[:], in_=query.rearrange("(p j) w -> p j w", j=PACK))
+        g_raw = sb.tile([P, PACK, Q], F32, name="g_raw")
+        nc.scalar.dma_start(out=g_raw[:], in_=gout.rearrange("(p j) w -> p j w", j=PACK))
         nc.scalar.activation(out=warm[:, 1:2], in_=warm[:, 0:1], func=ACT.Abs_reciprocal_sqrt)
-        nc.sync.dma_start(out=q_raw[:], in_=query.rearrange("(p j) w -> p j w", j=PACK))
-        nc.sync.dma_start(out=key_words[:].bitcast(I32), in_=keys_words[0].bitcast(I32))
+        val_words = sb.tile([P, T], U16, name="val_words", tag="vals_old", align_bytes=64)
         nc.sync.dma_start(out=val_words[:].bitcast(I32), in_=vals_words[0].bitcast(I32))
-        nc.sync.dma_start(out=g_raw[:], in_=gout.rearrange("(p j) w -> p j w", j=PACK))
         load_scale_rows(nc.sync, val_bytes, vals_scales)
-        olds = []
-        for c in range(T // STORE):
-            old_c = sb.tile([P, STORE], F32, name="old%d" % c)
-            nc.sync.dma_start(out=old_c[:], in_=old[:, slots(c * STORE, STORE)])
-            olds.append(old_c)
 
         def quantise(raw, name):
             grouped = sb.tile([P, Q, PACK], BF16, name=name + "_grouped", align_bytes=64)
@@ -91,22 +86,24 @@ def tile_attend_bpagestandard_s_kernel(tc, query, keys_words, keys_scales, gout,
 
         kw = sb.tile([P, I], U16, name="kw", align_bytes=64)
         kb = sb.tile([P, I], U8, name="kb", align_bytes=64)
-        nc.vector.tensor_copy(kb[:], listed(key_bytes, 0, I))
+        nc.vector.tensor_copy(kw[:], listed(key_words, 0, I))
         q_codes, q_scales = quantise(q_raw, "q")
         scores = []
         for h in range(2):
             sl = slots(h * HALF, HALF)
-            nc.vector.tensor_copy(kw[:, sl], listed(key_words, h * HALF, HALF))
+            nc.vector.tensor_copy(kb[:, sl], listed(key_bytes, h * HALF, HALF))
             a_h = ps.tile([P, HALF], F32, name="a%d" % h)
             nc.tensor.matmul_mx(out=a_h[:], lhsT=q_codes[:].bitcast(FP8X4), lhsT_scale=q_scales[:],
                                 rhs=kw[:, sl].bitcast(FP4X4), rhs_scale=kb[:, sl], start=True, stop=True)
             scores.append(a_h)
 
+        old_lo = sb.tile([P, T // 2], F32, name="old_lo", tag="keys_old", align_bytes=64)
+        nc.sync.dma_start(out=old_lo[:], in_=old[:, : T // 2])
         page_sum = sb.tile([P, G], F32, name="page_sum")
         page_sq = sb.tile([P, G], F32, name="page_sq")
         rinv = sb.tile([P, G], F32, name="rinv")
         ce = sb.tile([P, I], F32, name="ce", tag="ce_vb", align_bytes=64)
-        sq = sb.tile([P, I], F32, name="sq")
+        sq = sb.tile([P, I], F32, name="sq", tag="sq_vw", align_bytes=64)
         s = sb.tile([P, I], F32, name="s")
         p = sb.tile([P, I], F32, name="p")
         halves = [(slots(h * HALF, HALF), pages(h * HALF, HALF)) for h in range(2)]
@@ -125,26 +122,28 @@ def tile_attend_bpagestandard_s_kernel(tc, query, keys_words, keys_scales, gout,
         z = sb.tile([P, 1], F32, name="z")
         nc.vector.tensor_reduce(out=neg_max[:], in_=s[:], axis=AX.X, op=ALU.max, negate=True)
         nc.scalar.activation(out=p[:], in_=s[:], func=ACT.Exp, bias=neg_max[:], accum_out=z[:])
+        rz = sb.tile([P, 1], F32, name="rz")
+        rk = sb.tile([P, G], F32, name="rk")
+        nc.scalar.activation(out=rk[:], in_=rinv[:], func=ACT.Copy, scale=512.0)
+        nc.vector.reciprocal(out=rz[:], in_=z[:])
 
-        vw = sb.tile([P, I], U16, name="vw", align_bytes=64)
+        vw = sb.tile([P, I], U16, name="vw", tag="sq_vw", align_bytes=64)
         vb = sb.tile([P, I], U8, name="vb", tag="ce_vb", align_bytes=64)
         for h, (sl, pg) in enumerate(halves):
             nc.vector.tensor_copy(vw[:, sl], listed(val_words, h * HALF, HALF))
+        old_hi = sb.tile([P, T // 2], F32, name="old_hi", tag="vals_old", align_bytes=64)
+        nc.sync.dma_start(out=old_hi[:], in_=old[:, T // 2 :])
         g_codes, g_scales = quantise(g_raw, "g")
+        c0 = ps.tile([P, I], F32, name="c0")
         for h, (sl, pg) in enumerate(halves):
             nc.vector.tensor_copy(vb[:, sl], listed(val_bytes, h * HALF, HALF))
-        c0 = ps.tile([P, I], F32, name="c0")
-        nc.tensor.matmul_mx(out=c0[:], lhsT=g_codes[:].bitcast(FP8X4), lhsT_scale=g_scales[:],
-                            rhs=vw[:].bitcast(FP4X4), rhs_scale=vb[:], start=True, stop=True)
+            nc.tensor.matmul_mx(out=c0[:, sl], lhsT=g_codes[:].bitcast(FP8X4), lhsT_scale=g_scales[:],
+                                rhs=vw[:, sl].bitcast(FP4X4), rhs_scale=vb[:, sl], start=True, stop=True)
 
-        rz = sb.tile([P, 1], F32, name="rz")
         cbar = sb.tile([P, 1], F32, name="cbar")
-        rk = sb.tile([P, G], F32, name="rk")
         pr = sb.tile([P, I], F32, name="pr")
         cp = sb.tile([P, I], F32, name="cp")
-        nc.vector.reciprocal(out=rz[:], in_=z[:])
-        nc.vector.tensor_scalar(out=rk[:], in0=rinv[:], scalar1=rz[:], scalar2=512.0, op0=ALU.mult, op1=ALU.mult)
-        nc.vector.tensor_tensor(out=paged(pr[:]), in0=paged(p[:]), in1=spread(rk[:]), op=ALU.mult)
+        nc.vector.scalar_tensor_tensor(out=paged(pr[:]), in0=paged(p[:]), scalar=rz[:], in1=spread(rk[:]), op0=ALU.mult, op1=ALU.mult)
         nc.vector.scalar_tensor_tensor(out=cp[:], in0=c0[:], scalar=rz[:], in1=p[:], op0=ALU.mult, op1=ALU.mult, accum_out=cbar[:])
 
         dt = sb.tile([P, 2, I], F32, name="dt")
@@ -153,20 +152,20 @@ def tile_attend_bpagestandard_s_kernel(tc, query, keys_words, keys_scales, gout,
         y = sb.tile([P, I], F32, name="y")
         for sl, pg in halves:
             nc.vector.scalar_tensor_tensor(out=dt[:, 0, sl], in0=c0[:, sl], scalar=cbar[:], in1=pr[:, sl], op0=ALU.subtract, op1=ALU.mult)
+            nc.gpsimd.tensor_tensor(out=dt[:, 1, sl], in0=dt[:, 0, sl], in1=s[:, sl], op=ALU.mult)
         for sl, pg in halves:
-            nc.vector.tensor_tensor(out=dt[:, 1, sl], in0=dt[:, 0, sl], in1=s[:, sl], op=ALU.mult)
-        for u in range(4):
-            sl, pg = slots(u * QUARTER, QUARTER), pages(u * QUARTER, QUARTER)
-            nc.vector.tensor_reduce(out=sums[:, :, pg], in_=dt[:, :, sl].rearrange("p k (g j) -> p k g j", j=PAGE), axis=AX.X, op=ALU.add)
+            for k in range(2):
+                nc.vector.tensor_reduce(out=sums[:, k, pg], in_=paged(dt[:, k, sl]), axis=AX.X, op=ALU.add)
             nc.scalar.activation(out=means[:, :, pg], in_=sums[:, :, pg], func=ACT.Copy, scale=-1.0 / PAGE)
             for g in range(pg.start, pg.stop):
                 one = slots(g * PAGE, PAGE)
                 nc.scalar.activation(out=y[:, one], in_=s[:, one], func=ACT.Identity, scale=means[:, 1, g : g + 1], bias=means[:, 0, g : g + 1])
-        for u in range(4):
-            sl = slots(u * QUARTER, QUARTER)
-            nc.vector.tensor_tensor(out=listed(window, u * QUARTER, QUARTER), in0=dt[:, 0, sl], in1=y[:, sl], op=ALU.add)
+        for lo, n in ((0, FIRST), (FIRST, I - FIRST)):
+            sl = slots(lo, n)
+            nc.vector.tensor_tensor(out=listed(window, lo, n), in0=dt[:, 0, sl], in1=y[:, sl], op=ALU.add)
 
         for c in range(T // STORE):
             cols = slots(c * STORE, STORE)
-            nc.vector.tensor_tensor(out=olds[c][:], in0=window[:, cols], in1=olds[c][:], op=ALU.add)
-            nc.sync.dma_start(out=out[:, cols], in_=olds[c][:])
+            part = (old_lo, old_hi)[c // 2][:, slots(c % 2 * STORE, STORE)]
+            nc.vector.tensor_tensor(out=part, in0=window[:, cols], in1=part, op=ALU.add)
+            nc.sync.dma_start(out=out[:, cols], in_=part)

@@ -22,7 +22,8 @@ PACK = 4
 PAGE = I // G
 HALF = I // 2
 FIRST = 192
-STORE = 512
+PIECES = ((0, 128), (128, 128), (256, 256))
+STORES = (512, 512, 512, 512)
 
 
 def tile_attend_bpagestandard_s_kernel(tc, query, keys_words, keys_scales, gout, vals_words, vals_scales, old, offs, out):
@@ -30,6 +31,7 @@ def tile_attend_bpagestandard_s_kernel(tc, query, keys_words, keys_scales, gout,
 
     with ExitStack() as ctx:
         sb = ctx.enter_context(tc.tile_pool(name="sb", bufs=1))
+        reuse = ctx.enter_context(tc.tile_pool(name="reuse", bufs=1))
         ps = ctx.enter_context(tc.psum_pool(name="ps", bufs=1))
 
         def slots(lo, n):
@@ -49,7 +51,7 @@ def tile_attend_bpagestandard_s_kernel(tc, query, keys_words, keys_scales, gout,
         def listed(window, lo, n):
             return window[:].indirect(offsets[:, lo // 16 : (lo + n) // 16])
 
-        key_bytes = sb.tile([P, T], U8, name="key_bytes", align_bytes=64)
+        key_bytes = sb.tile([P, T], U8, name="key_bytes", tag="g_codes", align_bytes=64)
         val_bytes = sb.tile([P, T], U8, name="val_bytes", align_bytes=64)
         key_words = sb.tile([P, T], U16, name="key_words", tag="keys_old", align_bytes=64)
         q_raw = sb.tile([P, PACK, Q], F32, name="q_raw")
@@ -59,7 +61,7 @@ def tile_attend_bpagestandard_s_kernel(tc, query, keys_words, keys_scales, gout,
         nc.vector.memset(key_bytes[:].bitcast(I32), 0)
         nc.gpsimd.memset(warm[:, 0:1], 1.0)
         nc.gpsimd.memset(window[:], 0.0)
-        nc.vector.memset(val_bytes[:].bitcast(I32), 0)
+        nc.gpsimd.memset(val_bytes[:].bitcast(I32), 0)
 
         def load_scale_rows(queue, tile, rows):
             for f in range(4):
@@ -99,11 +101,11 @@ def tile_attend_bpagestandard_s_kernel(tc, query, keys_words, keys_scales, gout,
 
         old_lo = sb.tile([P, T // 2], F32, name="old_lo", tag="keys_old", align_bytes=64)
         nc.sync.dma_start(out=old_lo[:], in_=old[:, : T // 2])
-        page_sum = sb.tile([P, G], F32, name="page_sum")
+        page_sum = sb.tile([P, G], F32, name="page_sum", tag="sum_vw", align_bytes=64)
         page_sq = sb.tile([P, G], F32, name="page_sq")
         rinv = sb.tile([P, G], F32, name="rinv")
-        ce = sb.tile([P, I], F32, name="ce", tag="ce_vb", align_bytes=64)
-        sq = sb.tile([P, I], F32, name="sq", tag="sq_vw", align_bytes=64)
+        ce = reuse.tile([P, I], F32, name="ce", offset=0, align_bytes=64)
+        sq = sb.tile([P, I], F32, name="sq")
         s = sb.tile([P, I], F32, name="s")
         p = sb.tile([P, I], F32, name="p")
         halves = [(slots(h * HALF, HALF), pages(h * HALF, HALF)) for h in range(2)]
@@ -126,11 +128,14 @@ def tile_attend_bpagestandard_s_kernel(tc, query, keys_words, keys_scales, gout,
         rk = sb.tile([P, G], F32, name="rk")
         nc.scalar.activation(out=rk[:], in_=rinv[:], func=ACT.Copy, scale=512.0)
         nc.vector.reciprocal(out=rz[:], in_=z[:])
+        s16 = sb.tile([P, I], F32, name="s16")
+        nc.scalar.activation(out=s16[:], in_=s[:], func=ACT.Copy, scale=-1.0 / PAGE)
 
-        vw = sb.tile([P, I], U16, name="vw", tag="sq_vw", align_bytes=64)
-        vb = sb.tile([P, I], U8, name="vb", tag="ce_vb", align_bytes=64)
+        vw = [sb.tile([P, HALF], U16, name="vw0", tag="sum_vw", align_bytes=64),
+              reuse.tile([P, HALF], U16, name="vw1", offset=0, align_bytes=64)]
+        vb = reuse.tile([P, I], U8, name="vb", offset=512, align_bytes=64)
         for h, (sl, pg) in enumerate(halves):
-            nc.vector.tensor_copy(vw[:, sl], listed(val_words, h * HALF, HALF))
+            nc.vector.tensor_copy(vw[h][:], listed(val_words, h * HALF, HALF))
         old_hi = sb.tile([P, T // 2], F32, name="old_hi", tag="vals_old", align_bytes=64)
         nc.sync.dma_start(out=old_hi[:], in_=old[:, T // 2 :])
         g_codes, g_scales = quantise(g_raw, "g")
@@ -138,25 +143,34 @@ def tile_attend_bpagestandard_s_kernel(tc, query, keys_words, keys_scales, gout,
         for h, (sl, pg) in enumerate(halves):
             nc.vector.tensor_copy(vb[:, sl], listed(val_bytes, h * HALF, HALF))
             nc.tensor.matmul_mx(out=c0[:, sl], lhsT=g_codes[:].bitcast(FP8X4), lhsT_scale=g_scales[:],
-                                rhs=vw[:, sl].bitcast(FP4X4), rhs_scale=vb[:, sl], start=True, stop=True)
+                                rhs=vw[h][:].bitcast(FP4X4), rhs_scale=vb[:, sl], start=True, stop=True)
 
         cbar = sb.tile([P, 1], F32, name="cbar")
         pr = sb.tile([P, I], F32, name="pr")
         cp = sb.tile([P, I], F32, name="cp")
-        nc.vector.scalar_tensor_tensor(out=paged(pr[:]), in0=paged(p[:]), scalar=rz[:], in1=spread(rk[:]), op0=ALU.mult, op1=ALU.mult)
+        def weigh(sl, pg):
+            nc.vector.scalar_tensor_tensor(out=paged(pr[:, sl]), in0=paged(p[:, sl]), scalar=rz[:], in1=spread(rk[:, pg]), op0=ALU.mult, op1=ALU.mult)
+
+        weigh(*halves[0])
         nc.vector.scalar_tensor_tensor(out=cp[:], in0=c0[:], scalar=rz[:], in1=p[:], op0=ALU.mult, op1=ALU.mult, accum_out=cbar[:])
+        weigh(*halves[1])
 
         dt = sb.tile([P, 2, I], F32, name="dt")
-        sums = sb.tile([P, 2, G], F32, name="sums")
+        sums = sb.tile([P, G], F32, name="sums")
         means = sb.tile([P, 2, G], F32, name="means")
         y = sb.tile([P, I], F32, name="y")
         for sl, pg in halves:
             nc.vector.scalar_tensor_tensor(out=dt[:, 0, sl], in0=c0[:, sl], scalar=cbar[:], in1=pr[:, sl], op0=ALU.subtract, op1=ALU.mult)
-            nc.gpsimd.tensor_tensor(out=dt[:, 1, sl], in0=dt[:, 0, sl], in1=s[:, sl], op=ALU.mult)
-        for sl, pg in halves:
-            for k in range(2):
-                nc.vector.tensor_reduce(out=sums[:, k, pg], in_=paged(dt[:, k, sl]), axis=AX.X, op=ALU.add)
-            nc.scalar.activation(out=means[:, :, pg], in_=sums[:, :, pg], func=ACT.Copy, scale=-1.0 / PAGE)
+        for lo, n in PIECES:
+            sl = slots(lo, n)
+            nc.gpsimd.tensor_tensor(out=dt[:, 1, sl], in0=dt[:, 0, sl], in1=s16[:, sl], op=ALU.mult)
+        for lo, n in PIECES:
+            sl, pg = slots(lo, n), pages(lo, n)
+            if lo % HALF == 0:
+                hsl, hpg = halves[lo // HALF]
+                nc.vector.tensor_reduce(out=sums[:, hpg], in_=paged(dt[:, 0, hsl]), axis=AX.X, op=ALU.add)
+                nc.scalar.activation(out=means[:, 0, hpg], in_=sums[:, hpg], func=ACT.Copy, scale=-1.0 / PAGE)
+            nc.vector.tensor_reduce(out=means[:, 1, pg], in_=paged(dt[:, 1, sl]), axis=AX.X, op=ALU.add)
             for g in range(pg.start, pg.stop):
                 one = slots(g * PAGE, PAGE)
                 nc.scalar.activation(out=y[:, one], in_=s[:, one], func=ACT.Identity, scale=means[:, 1, g : g + 1], bias=means[:, 0, g : g + 1])
@@ -164,8 +178,11 @@ def tile_attend_bpagestandard_s_kernel(tc, query, keys_words, keys_scales, gout,
             sl = slots(lo, n)
             nc.vector.tensor_tensor(out=listed(window, lo, n), in0=dt[:, 0, sl], in1=y[:, sl], op=ALU.add)
 
-        for c in range(T // STORE):
-            cols = slots(c * STORE, STORE)
-            part = (old_lo, old_hi)[c // 2][:, slots(c % 2 * STORE, STORE)]
-            nc.vector.tensor_tensor(out=part, in0=window[:, cols], in1=part, op=ALU.add)
-            nc.sync.dma_start(out=out[:, cols], in_=part)
+        lo = 0
+        for n in STORES:
+            cols = slots(lo, n)
+            part = (old_lo, old_hi)[2 * lo // T][:, slots(lo % (T // 2), n)]
+            total = sb.tile([P, n], F32, name="total%d" % lo)
+            nc.vector.tensor_tensor(out=total[:], in0=window[:, cols], in1=part, op=ALU.add)
+            nc.sync.dma_start(out=out[:, cols], in_=total[:])
+            lo = lo + n

from contextlib import ExitStack

import concourse.mybir as mybir

D, E, T, I, Q, G = 512, 512, 2048, 512, 128, 32
FLOPS = 2 * Q * I * (D + E)

F32 = mybir.dt.float32
BF16 = mybir.dt.bfloat16
I32 = mybir.dt.int32
U32 = mybir.dt.uint32
U16 = mybir.dt.uint16
U8 = mybir.dt.uint8
FP8X4 = mybir.dt.float8_e4m3fn_x4
FP4X4 = mybir.dt.float4_e2m1fn_x4
ALU = mybir.AluOpType
ACT = mybir.ActivationFunctionType
AX = mybir.AxisListType

P = 128
PACK = 4
PAGE = I // G
HALF = I // 2
FIRST = 192
PIECES = ((0, 128), (128, 128), (256, 256))
STORES = (512, 512, 512, 512)


def tile_attend_bpagestandard_s_kernel(tc, query, keys_words, keys_scales, gout, vals_words, vals_scales, old, offs, out):
    nc = tc.nc

    with ExitStack() as ctx:
        sb = ctx.enter_context(tc.tile_pool(name="sb", bufs=1))
        reuse = ctx.enter_context(tc.tile_pool(name="reuse", bufs=1))
        ps = ctx.enter_context(tc.psum_pool(name="ps", bufs=1))

        def slots(lo, n):
            return slice(lo, lo + n)

        def pages(lo, n):
            return slice(lo // PAGE, (lo + n) // PAGE)

        def paged(ap):
            return ap.rearrange("p (g j) -> p g j", j=PAGE)

        def spread(ap):
            return ap.unsqueeze(2).to_broadcast([P, ap.shape[1], PAGE])

        offsets = sb.tile([P, I // 16], U16, name="offsets")

        def listed(window, lo, n):
            return window[:].indirect(offsets[:, lo // 16 : (lo + n) // 16])

        key_bytes = sb.tile([P, T], U8, name="key_bytes", tag="g_codes", align_bytes=64)
        val_bytes = sb.tile([P, T], U8, name="val_bytes", align_bytes=64)
        key_words = sb.tile([P, T], U16, name="key_words", tag="keys_old", align_bytes=64)
        q_raw = sb.tile([P, PACK, Q], F32, name="q_raw")
        window = sb.tile([P, T], F32, name="window")
        warm = sb.tile([P, 2], F32, name="warm", tag="vals_old", align_bytes=64)

        nc.vector.memset(key_bytes[:].bitcast(I32), 0)
        nc.gpsimd.memset(warm[:, 0:1], 1.0)
        nc.gpsimd.memset(window[:], 0.0)
        nc.gpsimd.memset(val_bytes[:].bitcast(I32), 0)

        def load_scale_rows(queue, tile, rows):
            for f in range(4):
                queue.dma_start(out=tile[32 * f : 32 * f + 4, :].bitcast(I32), in_=rows[0, 4 * f : 4 * f + 4, :].bitcast(I32))

        nc.sync.dma_start(offsets[:], offs)
        load_scale_rows(nc.sync, key_bytes, keys_scales)
        nc.scalar.dma_start(out=key_words[:].bitcast(I32), in_=keys_words[0].bitcast(I32))
        nc.scalar.dma_start(out=q_raw[:], in_=query.rearrange("(p j) w -> p j w", j=PACK))
        g_raw = sb.tile([P, PACK, Q], F32, name="g_raw")
        nc.scalar.dma_start(out=g_raw[:], in_=gout.rearrange("(p j) w -> p j w", j=PACK))
        nc.scalar.activation(out=warm[:, 1:2], in_=warm[:, 0:1], func=ACT.Abs_reciprocal_sqrt)
        val_words = sb.tile([P, T], U16, name="val_words", tag="vals_old", align_bytes=64)
        nc.sync.dma_start(out=val_words[:].bitcast(I32), in_=vals_words[0].bitcast(I32))
        load_scale_rows(nc.sync, val_bytes, vals_scales)

        def quantise(raw, name):
            grouped = sb.tile([P, Q, PACK], BF16, name=name + "_grouped", align_bytes=64)
            codes = sb.tile([P, Q], U32, name=name + "_codes", align_bytes=64)
            scales = sb.tile([P, Q], U8, name=name + "_scales", align_bytes=64)
            nc.scalar.copy(out=grouped[:], in_=raw[:].rearrange("p j w -> p w j"))
            nc.vector.quantize_mx(out=codes[:].bitcast(FP8X4), scales=scales[:], in_=grouped[:].rearrange("p w j -> p (w j)"))
            return codes, scales

        kw = sb.tile([P, I], U16, name="kw", align_bytes=64)
        kb = sb.tile([P, I], U8, name="kb", align_bytes=64)
        nc.vector.tensor_copy(kw[:], listed(key_words, 0, I))
        q_codes, q_scales = quantise(q_raw, "q")
        scores = []
        for h in range(2):
            sl = slots(h * HALF, HALF)
            nc.vector.tensor_copy(kb[:, sl], listed(key_bytes, h * HALF, HALF))
            a_h = ps.tile([P, HALF], F32, name="a%d" % h)
            nc.tensor.matmul_mx(out=a_h[:], lhsT=q_codes[:].bitcast(FP8X4), lhsT_scale=q_scales[:],
                                rhs=kw[:, sl].bitcast(FP4X4), rhs_scale=kb[:, sl], start=True, stop=True)
            scores.append(a_h)

        old_lo = sb.tile([P, T // 2], F32, name="old_lo", tag="keys_old", align_bytes=64)
        nc.sync.dma_start(out=old_lo[:], in_=old[:, : T // 2])
        page_sum = sb.tile([P, G], F32, name="page_sum", tag="sum_vw", align_bytes=64)
        page_sq = sb.tile([P, G], F32, name="page_sq")
        rinv = sb.tile([P, G], F32, name="rinv")
        ce = reuse.tile([P, I], F32, name="ce", offset=0, align_bytes=64)
        sq = sb.tile([P, I], F32, name="sq")
        s = sb.tile([P, I], F32, name="s")
        p = sb.tile([P, I], F32, name="p")
        halves = [(slots(h * HALF, HALF), pages(h * HALF, HALF)) for h in range(2)]
        for h, (sl, pg) in enumerate(halves):
            nc.vector.tensor_reduce(out=page_sum[:, pg], in_=paged(scores[h][:]), axis=AX.X, op=ALU.add)
        for h, (sl, pg) in enumerate(halves):
            nc.vector.scalar_tensor_tensor(out=paged(ce[:, sl]), in0=spread(page_sum[:, pg]), scalar=-1.0 / PAGE,
                                           in1=paged(scores[h][:]), op0=ALU.mult, op1=ALU.add)
            nc.scalar.activation(out=sq[:, sl], in_=ce[:, sl], func=ACT.Square)
        for sl, pg in halves:
            nc.vector.tensor_reduce(out=page_sq[:, pg], in_=paged(sq[:, sl]), axis=AX.X, op=ALU.add)
            nc.scalar.activation(out=rinv[:, pg], in_=page_sq[:, pg], func=ACT.Abs_reciprocal_sqrt, scale=1.0 / PAGE, bias=0.3)
        for sl, pg in halves:
            nc.vector.tensor_tensor(out=paged(s[:, sl]), in0=paged(ce[:, sl]), in1=spread(rinv[:, pg]), op=ALU.mult)
        neg_max = sb.tile([P, 1], F32, name="neg_max")
        z = sb.tile([P, 1], F32, name="z")
        nc.vector.tensor_reduce(out=neg_max[:], in_=s[:], axis=AX.X, op=ALU.max, negate=True)
        nc.scalar.activation(out=p[:], in_=s[:], func=ACT.Exp, bias=neg_max[:], accum_out=z[:])
        rz = sb.tile([P, 1], F32, name="rz")
        rk = sb.tile([P, G], F32, name="rk")
        nc.scalar.activation(out=rk[:], in_=rinv[:], func=ACT.Copy, scale=512.0)
        nc.vector.reciprocal(out=rz[:], in_=z[:])
        s16 = sb.tile([P, I], F32, name="s16")
        nc.scalar.activation(out=s16[:], in_=s[:], func=ACT.Copy, scale=-1.0 / PAGE)

        vw = [sb.tile([P, HALF], U16, name="vw0", tag="sum_vw", align_bytes=64),
              reuse.tile([P, HALF], U16, name="vw1", offset=0, align_bytes=64)]
        vb = reuse.tile([P, I], U8, name="vb", offset=512, align_bytes=64)
        for h, (sl, pg) in enumerate(halves):
            nc.vector.tensor_copy(vw[h][:], listed(val_words, h * HALF, HALF))
        old_hi = sb.tile([P, T // 2], F32, name="old_hi", tag="vals_old", align_bytes=64)
        nc.sync.dma_start(out=old_hi[:], in_=old[:, T // 2 :])
        g_codes, g_scales = quantise(g_raw, "g")
        c0 = ps.tile([P, I], F32, name="c0")
        for h, (sl, pg) in enumerate(halves):
            nc.vector.tensor_copy(vb[:, sl], listed(val_bytes, h * HALF, HALF))
            nc.tensor.matmul_mx(out=c0[:, sl], lhsT=g_codes[:].bitcast(FP8X4), lhsT_scale=g_scales[:],
                                rhs=vw[h][:].bitcast(FP4X4), rhs_scale=vb[:, sl], start=True, stop=True)

        cbar = sb.tile([P, 1], F32, name="cbar")
        pr = sb.tile([P, I], F32, name="pr")
        cp = sb.tile([P, I], F32, name="cp")
        def weigh(sl, pg):
            nc.vector.scalar_tensor_tensor(out=paged(pr[:, sl]), in0=paged(p[:, sl]), scalar=rz[:], in1=spread(rk[:, pg]), op0=ALU.mult, op1=ALU.mult)

        weigh(*halves[0])
        nc.vector.scalar_tensor_tensor(out=cp[:], in0=c0[:], scalar=rz[:], in1=p[:], op0=ALU.mult, op1=ALU.mult, accum_out=cbar[:])
        weigh(*halves[1])

        dt = sb.tile([P, 2, I], F32, name="dt")
        sums = sb.tile([P, G], F32, name="sums")
        means = sb.tile([P, 2, G], F32, name="means")
        y = sb.tile([P, I], F32, name="y")
        for sl, pg in halves:
            nc.vector.scalar_tensor_tensor(out=dt[:, 0, sl], in0=c0[:, sl], scalar=cbar[:], in1=pr[:, sl], op0=ALU.subtract, op1=ALU.mult)
        for lo, n in PIECES:
            sl = slots(lo, n)
            nc.gpsimd.tensor_tensor(out=dt[:, 1, sl], in0=dt[:, 0, sl], in1=s16[:, sl], op=ALU.mult)
        for lo, n in PIECES:
            sl, pg = slots(lo, n), pages(lo, n)
            if lo % HALF == 0:
                hsl, hpg = halves[lo // HALF]
                nc.vector.tensor_reduce(out=sums[:, hpg], in_=paged(dt[:, 0, hsl]), axis=AX.X, op=ALU.add)
                nc.scalar.activation(out=means[:, 0, hpg], in_=sums[:, hpg], func=ACT.Copy, scale=-1.0 / PAGE)
            nc.vector.tensor_reduce(out=means[:, 1, pg], in_=paged(dt[:, 1, sl]), axis=AX.X, op=ALU.add)
            for g in range(pg.start, pg.stop):
                one = slots(g * PAGE, PAGE)
                nc.scalar.activation(out=y[:, one], in_=s[:, one], func=ACT.Identity, scale=means[:, 1, g : g + 1], bias=means[:, 0, g : g + 1])
        for lo, n in ((0, FIRST), (FIRST, I - FIRST)):
            sl = slots(lo, n)
            nc.vector.tensor_tensor(out=listed(window, lo, n), in0=dt[:, 0, sl], in1=y[:, sl], op=ALU.add)

        lo = 0
        for n in STORES:
            cols = slots(lo, n)
            part = (old_lo, old_hi)[2 * lo // T][:, slots(lo % (T // 2), n)]
            total = sb.tile([P, n], F32, name="total%d" % lo)
            nc.vector.tensor_tensor(out=total[:], in0=window[:, cols], in1=part, op=ALU.add)
            nc.sync.dma_start(out=out[:, cols], in_=total[:])
            lo = lo + n
